import numpy as np
import ml_dtypes


def mxq(x, axis, fmt="e4m3"):
    dtype, down = {"e4m3": (ml_dtypes.float8_e4m3fn, 7), "e5m2": (ml_dtypes.float8_e5m2, 14)}[fmt]
    v = np.moveaxis(np.asarray(x, np.float32).astype(ml_dtypes.bfloat16).astype(np.float64), axis, -1)
    blocks = v.reshape(v.shape[:-1] + (-1, 32))
    amax = np.abs(blocks).max(-1, keepdims=True)
    byte = np.maximum(np.where(amax > 0, np.frexp(amax)[1] - 1 + 127, 0) - down, 1)
    scale = np.exp2(byte - 127.0)
    codes = (blocks / scale).astype(np.float32).astype(dtype).astype(np.float64)
    return np.moveaxis((codes * scale).reshape(v.shape), -1, axis)


WIDE = False


def mx_kscale(k):
    if not WIDE:
        return np.ones(k)
    levels = np.array([10, -10, 5, -5, 0])
    if k % 512:
        return np.exp2(np.random.permutation(np.resize(levels, k // 32))).repeat(32)
    a = np.empty((k // 512, 16))
    for p in range(k // 512):
        a[p, :8] = np.random.permutation(np.resize(levels, 8))
        for g in range(8):
            far = levels[np.abs(levels - a[p, g]) >= 10]
            a[p, g + 8] = far[np.random.randint(len(far))]
    return np.exp2(a.ravel()).repeat(32)


def f64(x):
    return np.asarray(x).astype(np.float64)


def striped(idx):
    return np.tile(idx.reshape(-1, 16).T, (8, 1)).astype(np.uint16)


def unstriped(offs):
    return offs[:16].T.reshape(-1).astype(np.int64)


E2M1 = np.array([0.0, 0.5, 1.0, 1.5, 2.0, 3.0, 4.0, 6.0, -0.0, -0.5, -1.0, -1.5, -2.0, -3.0, -4.0, -6.0])


def pack_weight(w, fmt):
    k, n = w.shape
    w = f64(np.asarray(w, np.float32).astype(ml_dtypes.bfloat16)).reshape(k // 32, 32, n)
    amax = np.abs(w).max(1)
    if fmt == "e4m3":
        byte = np.frexp(amax)[1] - 1 + 127 - 7
    else:
        mant, ex = np.frexp(amax / 6.0)
        byte = np.where(mant > 0.5, ex, ex - 1) + 127
    byte = np.clip(np.where(amax > 0, byte, 1), 1, 254)
    scaled = (w * np.exp2(127.0 - byte)[:, None, :]).reshape(k, n).astype(np.float32)
    by_word = np.ascontiguousarray(scaled.reshape(k // 512, 128, 4, n).transpose(0, 1, 3, 2))
    if fmt == "e4m3":
        words = by_word.astype(ml_dtypes.float8_e4m3fn).view(np.uint8)
    else:
        c = by_word.astype(ml_dtypes.float4_e2m1fn).view(np.uint8) & 0xF
        words = (c[..., 0::2] | (c[..., 1::2] << 4)).reshape(k // 512, 128, 2 * n)
    return np.ascontiguousarray(words), np.ascontiguousarray(byte.astype(np.uint8).reshape(k // 512, 16, n))


def unpack_weight(words, scales, fmt):
    g, _, n = scales.shape
    words = np.ascontiguousarray(words).reshape(g, 128, n, -1)
    if fmt == "e4m3":
        vals = words.view(ml_dtypes.float8_e4m3fn).astype(np.float64)
    else:
        nib = np.empty((g, 128, n, 4), np.uint8)
        nib[..., 0::2] = words & 0xF
        nib[..., 1::2] = words >> 4
        vals = E2M1[nib]
    vals = vals * np.repeat(np.exp2(scales.astype(np.float64) - 127.0), 8, axis=1)[..., None]
    return vals.transpose(0, 1, 3, 2).reshape(g * 512, n)


def relu(v):
    return np.maximum(v, 0.0)


K, T, E, N = 512, 1536, 12, 128
COUNTS = (128, 128, 128, 128, 384, 128, 256, 512, 128, 256, 512, 384)
STARTS = np.cumsum((0,) + COUNTS)


def by_expert(wq, xq):
    return np.concatenate([wq[e].T @ xq[:, STARTS[e]:STARTS[e + 1]] for e in range(E)], axis=1)


def setup_inputs():
    n = np.random.standard_normal
    s = mx_kscale(K)[:, None]
    both = np.repeat(np.arange(E), COUNTS)
    pair = np.stack([both[:T], both[T:]])[:, np.random.permutation(T)]
    pair = np.where(np.random.rand(T) < 0.5, pair, pair[::-1])
    for _ in range(8):
        s_, t_ = np.random.permutation(T).reshape(2, -1); r = np.random.randint(2, size=T // 2); q = np.random.randint(2, size=T // 2); x, y = pair[r, s_].copy(), pair[q, t_].copy()
        ok = (pair[1 - r, s_] != y) & (pair[1 - q, t_] != x); pair[r[ok], s_[ok]] = y[ok]; pair[q[ok], t_[ok]] = x[ok]
    order = np.argsort(pair.reshape(-1), kind="stable")
    slot_token = order % T; pos = np.empty(2 * T, np.int64); pos[order] = np.arange(2 * T); pos = pos.reshape(2, T)
    g = np.random.uniform(0.2, 0.8, T)
    w = [pack_weight(m, "e2m1") for m in n((E, K, N)) / np.sqrt(K) / s[None]]
    return {
        "xT": (n((K, T)) * s).astype(np.float32),
        "w_words": np.stack([m[0] for m in w]),
        "w_scales": np.stack([m[1] for m in w]),
        "b": (0.3 * n((N, E))).astype(np.float32),
        "gate": np.stack([np.tile(g, (N, 1)), np.tile(1.0 - g, (N, 1))]).astype(np.float32),
        "offs": striped(slot_token),
        "pos1": striped(pos[0]),
        "pos2": striped(pos[1]),
    }


def reference(xT, w_words, w_scales, b, gate, offs, pos1, pos2):
    idx = unstriped(offs)
    w = np.stack([unpack_weight(w_words[e], w_scales[e], "e2m1") for e in range(E)])
    xq = mxq(f64(xT)[:, idx], 0, "e4m3")
    y = by_expert(w, xq)
    y = relu(y + np.repeat(f64(b), COUNTS, axis=1))
    return f64(gate[0]) * y[:, unstriped(pos1)] + f64(gate[1]) * y[:, unstriped(pos2)]

@@ -1,0 +1,133 @@
+from contextlib import ExitStack
+
+import concourse.mybir as mybir
+
+K, T, E, N = 512, 1536, 12, 128
+COUNTS = (128, 128, 128, 128, 384, 128, 256, 512, 128, 256, 512, 384)
+S = 3072
+
+P = 128
+PACK = 4
+F32 = mybir.dt.float32
+BF16 = mybir.dt.bfloat16
+U32 = mybir.dt.uint32
+I32 = mybir.dt.int32
+U16 = mybir.dt.uint16
+U8 = mybir.dt.uint8
+E4M3X4 = mybir.dt.float8_e4m3fn_x4
+E2M1X4 = mybir.dt.float4_e2m1fn_x4
+RELU = mybir.ActivationFunctionType.Relu
+ADD = mybir.AluOpType.add
+MAX = mybir.AluOpType.max
+MULT = mybir.AluOpType.mult
+
+FLOPS = 2 * S * K * N
+
+CHUNKS = ((0, 512, 352), (512, 512, 352), (1024, 256, 176), (1280, 256, 176))
+CODE_GATHERS = ((0, 1152), (1152, 1152), (2304, 768))
+SCALE_GATHERS = ((0, 1024), (1024, 1152), (2176, 640), (2816, 256))
+PIECES = (
+    ((0, 0, 128, 0, 0), (1, 128, 128, 0, 128), (2, 256, 128, 0, 256), (3, 384, 128, 0, 384),
+     (4, 512, 384, 1, 0), (5, 896, 128, 1, 384)),
+    ((6, 1024, 256, 2, 0), (7, 1280, 512, 3, 0), (8, 1792, 128, 2, 256), (9, 1920, 256, 4, 0)),
+    ((10, 2176, 512, 5, 0), (11, 2688, 128, 4, 256)),
+    ((11, 2816, 128, 6, 0), (11, 2944, 128, 7, 0)),
+)
+OUT_SPLIT = ((0, 1024), (1024, 512))
+
+
+def widths(slots):
+    return {128: (128,), 256: (256,), 384: (256, 128), 512: (512,)}[slots]
+
+
+def tile_moe_rag_lin_relu_kernel(tc, xT, w_words, w_scales, b, gate, offs, pos1, pos2, out):
+    nc = tc.nc
+    with ExitStack() as ctx:
+        lists = ctx.enter_context(tc.tile_pool(name="lists", bufs=1))
+        keep = ctx.enter_context(tc.tile_pool(name="keep", bufs=1))
+        psum = ctx.enter_context(tc.psum_pool(name="psum", bufs=1))
+
+        idx = lists.tile([P, 2 * T // 16], U16, name="idx")
+        p1 = lists.tile([P, T // 16], U16, name="p1")
+        p2 = lists.tile([P, T // 16], U16, name="p2")
+
+        codes = keep.tile([P, T], U32, name="codes", align_bytes=64)
+        scales = keep.tile([P, T], U8, name="scales", align_bytes=64)
+        slot_codes = keep.tile([P, S], U32, name="slot_codes", align_bytes=64)
+        slot_scales = keep.tile([P, S], U8, name="slot_scales", align_bytes=64)
+        wt = keep.tile([P, E, 2 * N], U8, name="wt", align_bytes=64)
+        wt_scales = keep.tile([P, E, N], U8, name="wt_scales", align_bytes=64)
+        bias = keep.tile([P, E], F32, name="bias")
+        gates = keep.tile([P, 2, T], F32, name="gates")
+        y = keep.tile([P, S], F32, name="y")
+        first = keep.tile([P, T], F32, name="first")
+        second = keep.tile([P, T], F32, name="second")
+        total = keep.tile([P, T], F32, name="total")
+        warm = keep.tile([P, 1], F32, name="warm")
+
+        nc.gpsimd.memset(warm[:], 0.0)
+        nc.scalar.activation(warm[:], warm[:], RELU)
+        nc.gpsimd.memset(scales[:], 0)
+        nc.vector.memset(wt_scales[:].rearrange("p e n -> p (e n)").bitcast(I32), 0)
+
+        rows = xT.rearrange("(p j) t -> p j t", j=PACK)
+        raw = []
+        for i, (t0, n, v) in enumerate(CHUNKS):
+            r = keep.tile([P, PACK, n], F32, name=f"raw{i}")
+            nc.sync.dma_start(out=r[:], in_=rows[:, :, t0 : t0 + n])
+            raw.append(r)
+        nc.sync.dma_start(idx[:], offs)
+        w_scales_i = w_scales.bitcast(I32)
+        for q in range(4):
+            nc.sync.dma_start(
+                out=wt_scales[32 * q : 32 * q + 4].bitcast(I32),
+                in_=w_scales_i[:, 0, 4 * q : 4 * q + 4, :].rearrange("e q n -> q e n"),
+            )
+        nc.sync.dma_start(out=wt[:].bitcast(I32), in_=w_words.bitcast(I32).rearrange("e a p c -> p (e a) c"))
+        nc.sync.dma_start(out=bias[:], in_=b)
+        nc.sync.dma_start(p1[:], pos1)
+        nc.sync.dma_start(p2[:], pos2)
+        nc.sync.dma_start(out=gates[:], in_=gate.rearrange("c p t -> p c t"))
+
+        for i, (t0, n, v) in enumerate(CHUNKS):
+            g = keep.tile([P, n, PACK], BF16, name=f"grouped{i}", align_bytes=64)
+            nc.vector.tensor_copy(g[:, :v, :], raw[i][:, :, :v].rearrange("p j t -> p t j"))
+            nc.scalar.copy(g[:, v:, :], raw[i][:, :, v:].rearrange("p j t -> p t j"))
+            nc.vector.quantize_mx(
+                out=codes[:, t0 : t0 + n].bitcast(E4M3X4),
+                scales=scales[:, t0 : t0 + n],
+                in_=g[:].rearrange("p t j -> p (t j)"),
+            )
+
+        banks = [psum.tile([P, 512], F32, name=f"bank{i}") for i in range(8)]
+        for gi, (s0, n) in enumerate(SCALE_GATHERS):
+            if gi < len(CODE_GATHERS):
+                c0, m = CODE_GATHERS[gi]
+                nc.vector.tensor_copy(slot_codes[:, c0 : c0 + m], codes[:].indirect(idx[:, c0 // 16 : (c0 + m) // 16]))
+            nc.vector.tensor_copy(slot_scales[:, s0 : s0 + n], scales[:].indirect(idx[:, s0 // 16 : (s0 + n) // 16]))
+            for e, a, m, bank, c in PIECES[gi]:
+                d = 0
+                for w in widths(m):
+                    nc.tensor.matmul_mx(
+                        out=banks[bank][:, c + d : c + d + w],
+                        lhsT=wt[:, e, :].bitcast(E2M1X4),
+                        lhsT_scale=wt_scales[:, e, :],
+                        rhs=slot_codes[:, a + d : a + d + w].bitcast(E4M3X4),
+                        rhs_scale=slot_scales[:, a + d : a + d + w],
+                        start=True,
+                        stop=True,
+                    )
+                    d += w
+                if a + m == S:
+                    nc.vector.tensor_scalar(y[:, a : a + m], banks[bank][:, c : c + m], bias[:, e : e + 1], 0.0, ADD, MAX)
+                else:
+                    nc.scalar.activation(y[:, a : a + m], banks[bank][:, c : c + m], RELU, bias=bias[:, e : e + 1])
+
+        nc.vector.tensor_tensor(first[:], y[:].indirect(p1[:]), gates[:, 0, :], MULT)
+        for t0, n in OUT_SPLIT:
+            cols = slice(t0, t0 + n)
+            nc.vector.tensor_tensor(second[:, cols], y[:].indirect(p2[:, t0 // 16 : (t0 + n) // 16]), gates[:, 1, cols], MULT)
+        for t0, n in OUT_SPLIT:
+            cols = slice(t0, t0 + n)
+            nc.vector.tensor_tensor(total[:, cols], first[:, cols], second[:, cols], ADD)
+            nc.sync.dma_start(out=out[:, cols], in_=total[:, cols])

@@ -23,17 +23,17 @@ MULT = mybir.AluOpType.mult
 
 FLOPS = 2 * S * K * N
 
-CHUNKS = ((0, 512, 352), (512, 512, 352), (1024, 256, 176), (1280, 256, 176))
-CODE_GATHERS = ((0, 1152), (1152, 1152), (2304, 768))
-SCALE_GATHERS = ((0, 1024), (1024, 1152), (2176, 640), (2816, 256))
+CHUNKS = ((0, 512, 224), (512, 512, 224), (1024, 256, 112), (1280, 256, 128))
+CODE_GATHERS = ((0, 1024), (1024, 1152), (2176, 640), (2816, 256))
+SCALE_GATHERS = CODE_GATHERS
 PIECES = (
     ((0, 0, 128, 0, 0), (1, 128, 128, 0, 128), (2, 256, 128, 0, 256), (3, 384, 128, 0, 384),
      (4, 512, 384, 1, 0), (5, 896, 128, 1, 384)),
-    ((6, 1024, 256, 2, 0), (7, 1280, 512, 3, 0), (8, 1792, 128, 2, 256), (9, 1920, 256, 4, 0)),
-    ((10, 2176, 512, 5, 0), (11, 2688, 128, 4, 256)),
-    ((11, 2816, 128, 6, 0), (11, 2944, 128, 7, 0)),
+    ((6, 1024, 256, 2, 0), (8, 1792, 128, 2, 256), (7, 1280, 512, 3, 0), (9, 1920, 256, 4, 0)),
+    ((10, 2176, 512, 5, 0), (11, 2688, 128, 6, 0)),
+    ((11, 2816, 128, 7, 0), (11, 2944, 128, 0, 0)),
 )
-OUT_SPLIT = ((0, 1024), (1024, 512))
+OUT_SPLIT = ((0, 768), (768, 512), (1280, 256))
 
 
 def widths(slots):
@@ -89,15 +89,24 @@ def tile_moe_rag_lin_relu_kernel(tc, xT, w_words, w_scales, b, gate, offs, pos1,
         nc.sync.dma_start(p2[:], pos2)
         nc.sync.dma_start(out=gates[:], in_=gate.rearrange("c p t -> p c t"))
 
+        grouped = []
+
+        def quantize(i):
+            t0, n, v = CHUNKS[i]
+            nc.vector.quantize_mx(
+                out=codes[:, t0 : t0 + n].bitcast(E4M3X4),
+                scales=scales[:, t0 : t0 + n],
+                in_=grouped[i][:].rearrange("p t j -> p (t j)"),
+            )
+
         for i, (t0, n, v) in enumerate(CHUNKS):
             g = keep.tile([P, n, PACK], BF16, name=f"grouped{i}", align_bytes=64)
             nc.vector.tensor_copy(g[:, :v, :], raw[i][:, :, :v].rearrange("p j t -> p t j"))
             nc.scalar.copy(g[:, v:, :], raw[i][:, :, v:].rearrange("p j t -> p t j"))
-            nc.vector.quantize_mx(
-                out=codes[:, t0 : t0 + n].bitcast(E4M3X4),
-                scales=scales[:, t0 : t0 + n],
-                in_=g[:].rearrange("p t j -> p (t j)"),
-            )
+            grouped.append(g)
+            if i > 0:
+                quantize(i - 1)
+        quantize(len(CHUNKS) - 1)
 
         banks = [psum.tile([P, 512], F32, name=f"bank{i}") for i in range(8)]
         for gi, (s0, n) in enumerate(SCALE_GATHERS):
@@ -118,16 +127,20 @@ def tile_moe_rag_lin_relu_kernel(tc, xT, w_words, w_scales, b, gate, offs, pos1,
                         stop=True,
                     )
                     d += w
+            for e, a, m, bank, c in PIECES[gi]:
                 if a + m == S:
                     nc.vector.tensor_scalar(y[:, a : a + m], banks[bank][:, c : c + m], bias[:, e : e + 1], 0.0, ADD, MAX)
                 else:
                     nc.scalar.activation(y[:, a : a + m], banks[bank][:, c : c + m], RELU, bias=bias[:, e : e + 1])
 
         nc.vector.tensor_tensor(first[:], y[:].indirect(p1[:]), gates[:, 0, :], MULT)
-        for t0, n in OUT_SPLIT:
-            cols = slice(t0, t0 + n)
-            nc.vector.tensor_tensor(second[:, cols], y[:].indirect(p2[:, t0 // 16 : (t0 + n) // 16]), gates[:, 1, cols], MULT)
-        for t0, n in OUT_SPLIT:
-            cols = slice(t0, t0 + n)
-            nc.vector.tensor_tensor(total[:, cols], first[:, cols], second[:, cols], ADD)
-            nc.sync.dma_start(out=out[:, cols], in_=total[:, cols])
+        for i in range(len(OUT_SPLIT) + 1):
+            if i < len(OUT_SPLIT):
+                t0, n = OUT_SPLIT[i]
+                cols = slice(t0, t0 + n)
+                nc.vector.tensor_tensor(second[:, cols], y[:].indirect(p2[:, t0 // 16 : (t0 + n) // 16]), gates[:, 1, cols], MULT)
+            if i > 0:
+                t0, n = OUT_SPLIT[i - 1]
+                cols = slice(t0, t0 + n)
+                nc.vector.tensor_tensor(total[:, cols], first[:, cols], second[:, cols], ADD)
+                nc.sync.dma_start(out=out[:, cols], in_=total[:, cols])

@@ -23,7 +23,7 @@ MULT = mybir.AluOpType.mult
 
 FLOPS = 2 * S * K * N
 
-CHUNKS = ((0, 512, 224), (512, 512, 224), (1024, 256, 112), (1280, 256, 128))
+CHUNKS = ((0, 512, 224), (512, 512, 256), (1024, 256, 168), (1280, 128, 128), (1408, 128, 128))
 CODE_GATHERS = ((0, 1024), (1024, 1152), (2176, 640), (2816, 256))
 SCALE_GATHERS = CODE_GATHERS
 PIECES = (
@@ -33,7 +33,7 @@ PIECES = (
     ((10, 2176, 512, 5, 0), (11, 2688, 128, 6, 0)),
     ((11, 2816, 128, 7, 0), (11, 2944, 128, 0, 0)),
 )
-OUT_SPLIT = ((0, 768), (768, 512), (1280, 256))
+OUT_SPLIT = ((0, 960), (960, 352), (1312, 224))
 
 
 def widths(slots):
@@ -102,7 +102,8 @@ def tile_moe_rag_lin_relu_kernel(tc, xT, w_words, w_scales, b, gate, offs, pos1,
         for i, (t0, n, v) in enumerate(CHUNKS):
             g = keep.tile([P, n, PACK], BF16, name=f"grouped{i}", align_bytes=64)
             nc.vector.tensor_copy(g[:, :v, :], raw[i][:, :, :v].rearrange("p j t -> p t j"))
-            nc.scalar.copy(g[:, v:, :], raw[i][:, :, v:].rearrange("p j t -> p t j"))
+            if v < n:
+                nc.scalar.copy(g[:, v:, :], raw[i][:, :, v:].rearrange("p j t -> p t j"))
             grouped.append(g)
             if i > 0:
                 quantize(i - 1)

@@ -23,7 +23,8 @@ MULT = mybir.AluOpType.mult
 
 FLOPS = 2 * S * K * N
 
-CHUNKS = ((0, 512, 224), (512, 512, 256), (1024, 256, 168), (1280, 128, 128), (1408, 128, 128))
+LOADS = ((0, 1024), (1024, 256), (1280, 256))
+CHUNKS = ((0, 512, 304), (512, 512, 304), (1024, 256, 144), (1280, 256, 160))
 CODE_GATHERS = ((0, 1024), (1024, 1152), (2176, 640), (2816, 256))
 SCALE_GATHERS = CODE_GATHERS
 PIECES = (
@@ -72,10 +73,10 @@ def tile_moe_rag_lin_relu_kernel(tc, xT, w_words, w_scales, b, gate, offs, pos1,
 
         rows = xT.rearrange("(p j) t -> p j t", j=PACK)
         raw = []
-        for i, (t0, n, v) in enumerate(CHUNKS):
+        for i, (t0, n) in enumerate(LOADS):
             r = keep.tile([P, PACK, n], F32, name=f"raw{i}")
             nc.sync.dma_start(out=r[:], in_=rows[:, :, t0 : t0 + n])
-            raw.append(r)
+            raw += [(r, c0 - t0) for c0, m, v in CHUNKS if t0 <= c0 < t0 + n]
         nc.sync.dma_start(idx[:], offs)
         w_scales_i = w_scales.bitcast(I32)
         for q in range(4):
@@ -100,10 +101,10 @@ def tile_moe_rag_lin_relu_kernel(tc, xT, w_words, w_scales, b, gate, offs, pos1,
             )
 
         for i, (t0, n, v) in enumerate(CHUNKS):
+            r, c = raw[i]
             g = keep.tile([P, n, PACK], BF16, name=f"grouped{i}", align_bytes=64)
-            nc.vector.tensor_copy(g[:, :v, :], raw[i][:, :, :v].rearrange("p j t -> p t j"))
-            if v < n:
-                nc.scalar.copy(g[:, v:, :], raw[i][:, :, v:].rearrange("p j t -> p t j"))
+            nc.vector.tensor_copy(g[:, :v, :], r[:, :, c : c + v].rearrange("p j t -> p t j"))
+            nc.scalar.copy(g[:, v:, :], r[:, :, c + v : c + n].rearrange("p j t -> p t j"))
             grouped.append(g)
             if i > 0:
                 quantize(i - 1)

@@ -103,8 +103,12 @@ def tile_moe_rag_lin_relu_kernel(tc, xT, w_words, w_scales, b, gate, offs, pos1,
         for i, (t0, n, v) in enumerate(CHUNKS):
             r, c = raw[i]
             g = keep.tile([P, n, PACK], BF16, name=f"grouped{i}", align_bytes=64)
-            nc.vector.tensor_copy(g[:, :v, :], r[:, :, c : c + v].rearrange("p j t -> p t j"))
-            nc.scalar.copy(g[:, v:, :], r[:, :, c + v : c + n].rearrange("p j t -> p t j"))
+            nc.vector.tensor_copy(
+                g[:, :v, :].rearrange("p (q i) j -> p q j i", i=4), r[:, :, c : c + v].rearrange("p j (q i) -> p q j i", i=4)
+            )
+            nc.scalar.copy(
+                g[:, v:, :].rearrange("p (q i) j -> p q j i", i=4), r[:, :, c + v : c + n].rearrange("p j (q i) -> p q j i", i=4)
+            )
             grouped.append(g)
             if i > 0:
                 quantize(i - 1)

from contextlib import ExitStack

import concourse.mybir as mybir

K, T, E, N = 512, 1536, 12, 128
COUNTS = (128, 128, 128, 128, 384, 128, 256, 512, 128, 256, 512, 384)
S = 3072

P = 128
PACK = 4
F32 = mybir.dt.float32
BF16 = mybir.dt.bfloat16
U32 = mybir.dt.uint32
I32 = mybir.dt.int32
U16 = mybir.dt.uint16
U8 = mybir.dt.uint8
E4M3X4 = mybir.dt.float8_e4m3fn_x4
E2M1X4 = mybir.dt.float4_e2m1fn_x4
RELU = mybir.ActivationFunctionType.Relu
ADD = mybir.AluOpType.add
MAX = mybir.AluOpType.max
MULT = mybir.AluOpType.mult

FLOPS = 2 * S * K * N

LOADS = ((0, 1024), (1024, 256), (1280, 256))
CHUNKS = ((0, 512, 304), (512, 512, 304), (1024, 256, 144), (1280, 256, 160))
CODE_GATHERS = ((0, 1024), (1024, 1152), (2176, 640), (2816, 256))
SCALE_GATHERS = CODE_GATHERS
PIECES = (
    ((0, 0, 128, 0, 0), (1, 128, 128, 0, 128), (2, 256, 128, 0, 256), (3, 384, 128, 0, 384),
     (4, 512, 384, 1, 0), (5, 896, 128, 1, 384)),
    ((6, 1024, 256, 2, 0), (8, 1792, 128, 2, 256), (7, 1280, 512, 3, 0), (9, 1920, 256, 4, 0)),
    ((10, 2176, 512, 5, 0), (11, 2688, 128, 6, 0)),
    ((11, 2816, 128, 7, 0), (11, 2944, 128, 0, 0)),
)
OUT_SPLIT = ((0, 960), (960, 352), (1312, 224))


def widths(slots):
    return {128: (128,), 256: (256,), 384: (256, 128), 512: (512,)}[slots]


def tile_moe_rag_lin_relu_kernel(tc, xT, w_words, w_scales, b, gate, offs, pos1, pos2, out):
    nc = tc.nc
    with ExitStack() as ctx:
        lists = ctx.enter_context(tc.tile_pool(name="lists", bufs=1))
        keep = ctx.enter_context(tc.tile_pool(name="keep", bufs=1))
        psum = ctx.enter_context(tc.psum_pool(name="psum", bufs=1))

        idx = lists.tile([P, 2 * T // 16], U16, name="idx")
        p1 = lists.tile([P, T // 16], U16, name="p1")
        p2 = lists.tile([P, T // 16], U16, name="p2")

        codes = keep.tile([P, T], U32, name="codes", align_bytes=64)
        scales = keep.tile([P, T], U8, name="scales", align_bytes=64)
        slot_codes = keep.tile([P, S], U32, name="slot_codes", align_bytes=64)
        slot_scales = keep.tile([P, S], U8, name="slot_scales", align_bytes=64)
        wt = keep.tile([P, E, 2 * N], U8, name="wt", align_bytes=64)
        wt_scales = keep.tile([P, E, N], U8, name="wt_scales", align_bytes=64)
        bias = keep.tile([P, E], F32, name="bias")
        gates = keep.tile([P, 2, T], F32, name="gates")
        y = keep.tile([P, S], F32, name="y")
        first = keep.tile([P, T], F32, name="first")
        second = keep.tile([P, T], F32, name="second")
        total = keep.tile([P, T], F32, name="total")
        warm = keep.tile([P, 1], F32, name="warm")

        nc.gpsimd.memset(warm[:], 0.0)
        nc.scalar.activation(warm[:], warm[:], RELU)
        nc.gpsimd.memset(scales[:], 0)
        nc.vector.memset(wt_scales[:].rearrange("p e n -> p (e n)").bitcast(I32), 0)

        rows = xT.rearrange("(p j) t -> p j t", j=PACK)
        raw = []
        for i, (t0, n) in enumerate(LOADS):
            r = keep.tile([P, PACK, n], F32, name=f"raw{i}")
            nc.sync.dma_start(out=r[:], in_=rows[:, :, t0 : t0 + n])
            raw += [(r, c0 - t0) for c0, m, v in CHUNKS if t0 <= c0 < t0 + n]
        nc.sync.dma_start(idx[:], offs)
        w_scales_i = w_scales.bitcast(I32)
        for q in range(4):
            nc.sync.dma_start(
                out=wt_scales[32 * q : 32 * q + 4].bitcast(I32),
                in_=w_scales_i[:, 0, 4 * q : 4 * q + 4, :].rearrange("e q n -> q e n"),
            )
        nc.sync.dma_start(out=wt[:].bitcast(I32), in_=w_words.bitcast(I32).rearrange("e a p c -> p (e a) c"))
        nc.sync.dma_start(out=bias[:], in_=b)
        nc.sync.dma_start(p1[:], pos1)
        nc.sync.dma_start(p2[:], pos2)
        nc.sync.dma_start(out=gates[:], in_=gate.rearrange("c p t -> p c t"))

        grouped = []

        def quantize(i):
            t0, n, v = CHUNKS[i]
            nc.vector.quantize_mx(
                out=codes[:, t0 : t0 + n].bitcast(E4M3X4),
                scales=scales[:, t0 : t0 + n],
                in_=grouped[i][:].rearrange("p t j -> p (t j)"),
            )

        for i, (t0, n, v) in enumerate(CHUNKS):
            r, c = raw[i]
            g = keep.tile([P, n, PACK], BF16, name=f"grouped{i}", align_bytes=64)
            nc.vector.tensor_copy(
                g[:, :v, :].rearrange("p (q i) j -> p q j i", i=4), r[:, :, c : c + v].rearrange("p j (q i) -> p q j i", i=4)
            )
            nc.scalar.copy(
                g[:, v:, :].rearrange("p (q i) j -> p q j i", i=4), r[:, :, c + v : c + n].rearrange("p j (q i) -> p q j i", i=4)
            )
            grouped.append(g)
            if i > 0:
                quantize(i - 1)
        quantize(len(CHUNKS) - 1)

        banks = [psum.tile([P, 512], F32, name=f"bank{i}") for i in range(8)]
        for gi, (s0, n) in enumerate(SCALE_GATHERS):
            if gi < len(CODE_GATHERS):
                c0, m = CODE_GATHERS[gi]
                nc.vector.tensor_copy(slot_codes[:, c0 : c0 + m], codes[:].indirect(idx[:, c0 // 16 : (c0 + m) // 16]))
            nc.vector.tensor_copy(slot_scales[:, s0 : s0 + n], scales[:].indirect(idx[:, s0 // 16 : (s0 + n) // 16]))
            for e, a, m, bank, c in PIECES[gi]:
                d = 0
                for w in widths(m):
                    nc.tensor.matmul_mx(
                        out=banks[bank][:, c + d : c + d + w],
                        lhsT=wt[:, e, :].bitcast(E2M1X4),
                        lhsT_scale=wt_scales[:, e, :],
                        rhs=slot_codes[:, a + d : a + d + w].bitcast(E4M3X4),
                        rhs_scale=slot_scales[:, a + d : a + d + w],
                        start=True,
                        stop=True,
                    )
                    d += w
            for e, a, m, bank, c in PIECES[gi]:
                if a + m == S:
                    nc.vector.tensor_scalar(y[:, a : a + m], banks[bank][:, c : c + m], bias[:, e : e + 1], 0.0, ADD, MAX)
                else:
                    nc.scalar.activation(y[:, a : a + m], banks[bank][:, c : c + m], RELU, bias=bias[:, e : e + 1])

        nc.vector.tensor_tensor(first[:], y[:].indirect(p1[:]), gates[:, 0, :], MULT)
        for i in range(len(OUT_SPLIT) + 1):
            if i < len(OUT_SPLIT):
                t0, n = OUT_SPLIT[i]
                cols = slice(t0, t0 + n)
                nc.vector.tensor_tensor(second[:, cols], y[:].indirect(p2[:, t0 // 16 : (t0 + n) // 16]), gates[:, 1, cols], MULT)
            if i > 0:
                t0, n = OUT_SPLIT[i - 1]
                cols = slice(t0, t0 + n)
                nc.vector.tensor_tensor(total[:, cols], first[:, cols], second[:, cols], ADD)
                nc.sync.dma_start(out=out[:, cols], in_=total[:, cols])
